import numpy as np, ml_dtypes
CORES = [12,28,60,100,156,228]
N = 6
import mx_ref
NC, G = 128, 4
BF = ml_dtypes.bfloat16
def cut(t, i, w=512):
    return t[:, w * i:w * i + w]
def tile(rs):
    return np.stack(rs, axis=2).reshape(128, -1).astype(BF)
def layer(w, X):
    out = []
    for i in range(G):
        for t in range(len(X)):
            p = mx_ref.matmul(mx_ref.quantize(cut(w, len(X) * i + t)), X[t])
            z = p if t == 0 else z + p
        out.append(z)
    return out
def scaled(Z, s):
    return [z * s for z in Z]
def setup_inputs(rng):
    def f(*shape):
        return mx_ref.flush((rng.standard_normal(shape, dtype=np.float32) * np.exp2(rng.integers(-2, 3, shape[:-1] + (1,)))).astype(BF))
    return {"x": f(N, 128, 4 * NC), "w1": f(N, 128, G * 512), "w2": f(N, 128, 512)}
def setup_inputs_blocks(rng):
    d = setup_inputs(rng)
    for k in ("w2",): d[k] = mx_ref.spread(d[k], rng, 4)
    for k in ("x", "w1"): d[k] = mx_ref.spread(d[k], rng, 2)
    return d
def setup_inputs_wide(rng):
    d = setup_inputs(rng)
    for k in ("x", "w1", "w2"): d[k] = mx_ref.flush((d[k].astype(np.float32) * np.exp2(rng.integers(-3, 4, (N, 1, 1))).astype(np.float32)).astype(BF))
    return d
def reference(x, w1, w2, own=None):
    Z = [layer(w1[r], [mx_ref.quantize(x[r])]) for r in range(N)]
    a = max(float(np.abs(z).max()) for r in range(N) for z in Z[r])
    s = np.float32(1 / a)
    h = np.stack([tile(scaled(Z[r], s)) for r in range(N)])
    use = h if own is None else own["h"]
    H = [mx_ref.quantize(use[j]) for j in range(N)]
    y = np.zeros((N, 128, N * NC), np.float32)
    for r in range(N):
        qw = mx_ref.quantize(w2[r])
        for j in range(N):
            y[r][:, NC * j:NC * j + NC] = mx_ref.matmul(qw, H[j])
    return {"h": h, "y": y}

@@ -1,0 +1,249 @@
+from concourse.bass import DstId, RemoteDMATransfer
+from concourse.mybir import dt, AluOpType, AxisListType, ActivationFunctionType
+
+N, NC, G = 6, 128, 4
+W = 4 * NC
+SCRATCH = {
+    "xb": ("sbuf", [128, W], "bfloat16"),
+    "w1b": ("sbuf", [128, G * W], "bfloat16"),
+    "w2b": ("sbuf", [128, W], "bfloat16"),
+    "xq": ("sbuf", [128, NC], "float8_e4m3fn_x4"),
+    "xs": ("sbuf", [128, NC], "uint8"),
+    "wq": ("sbuf", [128, G * NC], "float8_e4m3fn_x4"),
+    "ws": ("sbuf", [128, G * NC], "uint8"),
+    "vq": ("sbuf", [128, NC], "float8_e4m3fn_x4"),
+    "vs": ("sbuf", [128, NC], "uint8"),
+    "ones": ("sbuf", [128, 128], "float32"),
+    "ident": ("sbuf", [128, 128], "float32"),
+    "diag": ("sbuf", [128, 128], "float32"),
+    "part": ("sbuf", [128, G], "float32"),
+    "vmax": ("sbuf", [128, 4], "float32"),
+    "amax": ("sbuf", [128, 12], "float32"),
+    "big": ("sbuf", [128, 4], "float32"),
+    "s": ("sbuf", [128, 4], "float32"),
+    "hb": ("sbuf", [128, W], "bfloat16"),
+    "hq": ("sbuf", [128, NC], "float8_e4m3fn_x4"),
+    "hs": ("sbuf", [128, NC], "uint8"),
+    "lc": ("sbuf", [128, N * NC], "float8_e4m3fn_x4"),
+    "lp": ("sbuf", [128, N * NC], "uint8"),
+    "rm": ("sbuf", [128, 4], "float32"),
+    "rc": ("sbuf", [128, NC], "float8_e4m3fn_x4"),
+    "rp": ("sbuf", [128, NC], "uint8"),
+    "yb": ("sbuf", [128, N * NC], "float32"),
+    "ps": ("psum", [128, 4096], "float32"),
+}
+SEMAPHORES = (["l_x", "l_wa", "l_wb", "l_w2", "q_x", "q_w0", "q_w1", "q_w2", "q_w3", "q_v", "q_h",
+               "z0", "z1", "z2", "z3", "ones", "zero", "ident", "part", "vmax", "diag", "bc", "own",
+               "big", "s", "hv", "hsc", "m_in", "sent", "st", "rm_in", "rc_in", "rp_in"]
+              + ["arr%d" % j for j in range(N)] + ["y%d" % j for j in range(N)] + ["c%d" % j for j in range(N)])
+
+
+def count(mask):
+    return bin(mask).count("1")
+
+
+def routes(T, topo, r):
+    me = T.cores[r]
+    others = [j for j in range(N) if j != r]
+    near = [j for j in others if topo.may_write(me, T.cores[j])]
+    far = [j for j in others if j not in near]
+    chip = [c for c in range(256) if c != me and topo.host(c) == topo.host(me) and topo.chip(c) == topo.chip(me)]
+    rel = [c for c in chip if all(topo.may_write(c, T.cores[j]) for j in far)]
+    a = [c for c in rel if topo.die(c) == topo.die(me)]
+    b = [c for c in rel if topo.die(c) != topo.die(me)]
+    if sorted(near + [r]).index(r) % 2:
+        a, b = b, a
+    if len(far) > 2:
+        m = list(zip([a[0], b[0], a[1], b[1]], [[j] for j in far]))
+        c = [(a[0], far[:2]), (b[0], far[2:])]
+        p = [(b[1], far[:2]), (a[1], far[2:])]
+    else:
+        m = [(a[0], far[:1]), (b[0], far[1:])]
+        c = [(a[0], far)]
+        p = [(b[0], far)]
+    return near, far, m, c, p
+
+
+def dst(topo, src, d):
+    rid, pid = topo.addr(d, src)
+    return DstId(rid=rid, pnc=pid)
+
+
+def xfer(topo, core, src, dests, mask, sem):
+    return RemoteDMATransfer(dst_ids=[dst(topo, core, d) for d, _ in dests], dma_engine_mask=mask, remote_sem=sem,
+                             srcs=[src], dsts=[v for _, v in dests])
+
+
+def mcol(T, d, r):
+    k = 4 + (r if r < d else r - 1)
+    return T.amax[:, k:k + 1]
+
+
+def codes(v):
+    return v.bitcast(dt.uint8)
+
+
+def blk(t, j):
+    return t[:, NC * j:NC * j + NC]
+
+
+def relay_program(g, core, T, topo):
+    for r in range(N):
+        near, far, m, c, p = routes(T, topo, r)
+        me = T.cores[r]
+        sent = 0
+        on = topo.mask(me, core) if me != core else 0
+        for kind, table in (("m", m), ("c", c), ("p", p)):
+            for rc, dests in table:
+                if rc != core:
+                    continue
+                off = topo.mask(core, T.cores[dests[0]])
+                if kind == "m":
+                    g.wait_ge(T.sem.rm_in, count(hand_mask(T, topo, r, core)))
+                    t = xfer(topo, core, T.rm[:, 0:1], [(T.cores[d], mcol(T, d, r)) for d in dests], off, T.sem.m_in)
+                elif kind == "c":
+                    g.wait_ge(T.sem.rc_in, count(hand_mask(T, topo, r, core)))
+                    t = xfer(topo, core, codes(T.rc[:, :]), [(T.cores[d], codes(blk(T.lc, r))) for d in dests], off,
+                             T.sem["arr%d" % r])
+                else:
+                    g.wait_ge(T.sem.rp_in, count(hand_mask(T, topo, r, core)))
+                    t = xfer(topo, core, T.rp[:, :], [(T.cores[d], blk(T.lp, r)) for d in dests], off,
+                             T.sem["arr%d" % r])
+                g.remote_dma_fused([t], local_sem=T.sem.sent)
+                sent += count(off)
+        if sent:
+            g.wait_ge(T.sem.sent, sent)
+
+
+def hand_mask(T, topo, r, relay):
+    near, far, m, c, p = routes(T, topo, r)
+    on = topo.mask(T.cores[r], relay)
+    off = topo.mask(T.cores[r], T.cores[near[0]])
+    return on if len(far) > len(near) else on & ~off
+
+
+def rank_program(g, core, T, topo):
+    rank = T.rank_of(core)
+    if rank is None:
+        relay_program(g, core, T, topo)
+        return
+    S = T.sem
+    near, far, m, c, p = routes(T, topo, rank)
+    off = topo.mask(core, T.cores[near[0]])
+    hand = hand_mask(T, topo, rank, m[0][0])
+    order = [rank] + near + far
+    X, V, A, E, Y = AxisListType.X, g.vector, g.scalar, g.tensor, g.sync
+    mult, mx = AluOpType.mult, AluOpType.max
+    half = G // 2 * W
+
+    Y.dma_start(T.xb[:, :], T.x[:, :]).then_inc(S.l_x, 16)
+    A.dma_start(T.w1b[:, 0:half], T.w1[:, 0:half]).then_inc(S.l_wa, 16)
+    Y.dma_start(T.w1b[:, half:2 * half], T.w1[:, half:2 * half]).then_inc(S.l_wb, 16)
+    Y.wait_ge(S.l_wb, 16)
+    Y.dma_start(T.w2b[:, :], T.w2[:, :]).then_inc(S.l_w2, 16)
+
+    V.memset(T.ones[:, :], 1.0).then_inc(S.ones, 1)
+    V.memset(T.amax[:, 0:4], 0.0).then_inc(S.zero, 1)
+    g.wait_ge(S.ones, 1)
+    g.affine_select(T.ident[:, :], T.ones[:, :], [[-1, 128]], AluOpType.is_equal, 0.0, 0, 1).then_inc(S.ident, 1)
+
+    def quant_w(i):
+        V.quantize_mx(blk(T.wq, i), blk(T.ws, i), T.w1b[:, W * i:W * i + W]).then_inc(S["q_w%d" % i], 1)
+
+    def reduce_z(i):
+        V.wait_ge(S["z%d" % i], 1)
+        V.tensor_reduce(T.part[:, i:i + 1], T.ps[:, 512 * i:512 * i + NC], X, mx,
+                        apply_absolute_value=True).then_inc(S.part, 1)
+
+    V.wait_ge(S.l_x, 16)
+    V.quantize_mx(T.xq[:, :], T.xs[:, :], T.xb[:, :]).then_inc(S.q_x, 1)
+    V.wait_ge(S.l_wa, 16)
+    quant_w(0)
+    quant_w(1)
+    reduce_z(0)
+    reduce_z(1)
+    V.wait_ge(S.l_wb, 16)
+    quant_w(2)
+    quant_w(3)
+    reduce_z(2)
+    reduce_z(3)
+    V.wait_ge(S.part, G)
+    V.tensor_reduce(T.vmax[:, 0:1], T.part[:, 0:G], X, mx).then_inc(S.vmax, 1)
+    V.wait_ge(S.vmax, 1)
+    V.wait_ge(S.ident, 1)
+    V.tensor_scalar(T.diag[:, :], T.ident[:, :], T.vmax[:, 0:1], None, mult).then_inc(S.diag, 1)
+
+    E.wait_ge(S.q_x, 1)
+    for i in range(G):
+        E.wait_ge(S["q_w%d" % i], 1)
+        E.matmul_mx(T.ps[:, 512 * i:512 * i + NC], blk(T.wq, i), blk(T.ws, i), T.xq[:, :], T.xs[:, :],
+                    True, True).then_inc(S["z%d" % i], 1)
+    E.wait_ge(S.ones, 1)
+    E.wait_ge(S.diag, 1)
+    E.matmul(T.ps[:, 2048:2048 + 128], T.ones[:, :], T.diag[:, :], True, True).then_inc(S.bc, 1)
+
+    V.wait_ge(S.bc, 1)
+    V.wait_ge(S.zero, 1)
+    V.tensor_reduce(T.amax[:, 0:1], T.ps[:, 2048:2048 + 128], X, mx).then_inc(S.own, 1)
+
+    sent = 0
+    g.wait_ge(S.own, 1)
+    g.remote_dma_fused([xfer(topo, core, T.amax[:, 0:1], [(k, T.rm[:, 0:1]) for k, _ in m], hand, S.rm_in)],
+                       local_sem=S.sent)
+    g.remote_dma_fused([xfer(topo, core, T.amax[:, 0:1], [(T.cores[d], mcol(T, d, rank)) for d in near], off, S.m_in)],
+                       local_sem=S.sent)
+    sent += count(hand) + count(off)
+
+    V.wait_ge(S.l_w2, 16)
+    V.quantize_mx(T.vq[:, :], T.vs[:, :], T.w2b[:, :]).then_inc(S.q_v, 1)
+
+    V.wait_ge(S.own, 1)
+    V.wait_ge(S.m_in, sum(count(topo.mask(T.cores[j], core)) for j in near) + sum(count(off) for j in far))
+    V.tensor_reduce(T.big[:, 0:1], T.amax[:, 0:4 + N - 1], X, mx).then_inc(S.big, 1)
+    V.wait_ge(S.big, 1)
+    V.reciprocal(T.s[:, 0:1], T.big[:, 0:1]).then_inc(S.s, 1)
+    V.wait_ge(S.s, 1)
+    A.wait_ge(S.s, 1)
+    for b in (0, 1):
+        V.tensor_scalar(T.hb[:, b:W:G], T.ps[:, 512 * b:512 * b + NC], T.s[:, 0:1], None, mult).then_inc(S.hv, 1)
+    for b in (2, 3):
+        A.wait_ge(S["z%d" % b], 1)
+        A.activation(T.hb[:, b:W:G], T.ps[:, 512 * b:512 * b + NC], ActivationFunctionType.Copy,
+                     scale=T.s[:, 0:1]).then_inc(S.hsc, 1)
+    V.wait_ge(S.hv, 2)
+    V.wait_ge(S.hsc, 2)
+    V.quantize_mx(T.hq[:, :], T.hs[:, :], T.hb[:, :]).then_inc(S.q_h, 1)
+    Y.wait_ge(S.hv, 2)
+    Y.wait_ge(S.hsc, 2)
+    Y.dma_start(T.h[:, :], T.hb[:, :]).then_inc(S.st, 16)
+
+    g.wait_ge(S.q_h, 1)
+    hq, hs = codes(T.hq[:, :]), T.hs[:, :]
+    arr = S["arr%d" % rank]
+    tc = xfer(topo, core, hq, [(k, codes(T.rc[:, :])) for k, _ in c], hand, S.rc_in)
+    tp = xfer(topo, core, hs, [(k, T.rp[:, :]) for k, _ in p], hand, S.rp_in)
+    nc = xfer(topo, core, hq, [(T.cores[d], codes(blk(T.lc, rank))) for d in near], off, arr)
+    np_ = xfer(topo, core, hs, [(T.cores[d], blk(T.lp, rank)) for d in near], off, arr)
+    calls = [[tc, nc], [tp, np_]] if hand & off == 0 else [[tc], [tp], [nc], [np_]]
+    for call in calls:
+        g.remote_dma_fused(call, local_sem=S.sent)
+    sent += 2 * count(hand) + 2 * count(off)
+
+    E.wait_ge(S.q_v, 1)
+    E.wait_ge(S.q_h, 1)
+    for k, j in enumerate(order):
+        bank = 512 * ((5 + k) % 8)
+        if j != rank:
+            E.wait_ge(S["arr%d" % j], 2 * count(off))
+        qc, qs = (T.hq[:, :], T.hs[:, :]) if j == rank else (blk(T.lc, j), blk(T.lp, j))
+        E.matmul_mx(T.ps[:, bank:bank + NC], T.vq[:, :], T.vs[:, :], qc, qs, True, True).then_inc(S["y%d" % k], 1)
+        q = V if k % 2 == 0 else A
+        q.wait_ge(S["y%d" % k], 1)
+        if k % 2 == 0:
+            V.tensor_copy(blk(T.yb, j), T.ps[:, bank:bank + NC]).then_inc(S["c%d" % k], 1)
+        else:
+            A.activation(blk(T.yb, j), T.ps[:, bank:bank + NC], ActivationFunctionType.Copy).then_inc(S["c%d" % k], 1)
+        Y.wait_ge(S["c%d" % k], 1)
+        Y.dma_start(blk(T.y, j), blk(T.yb, j)).then_inc(S.st, 16)
+    Y.wait_ge(S.st, 16 * (N + 1))
+    g.wait_ge(S.sent, sent)

@@ -14,9 +14,10 @@ SCRATCH = {
     "vq": ("sbuf", [128, NC], "float8_e4m3fn_x4"),
     "vs": ("sbuf", [128, NC], "uint8"),
     "ones": ("sbuf", [128, 128], "float32"),
-    "ident": ("sbuf", [128, 128], "float32"),
-    "diag": ("sbuf", [128, 128], "float32"),
-    "part": ("sbuf", [128, G], "float32"),
+    "pick": ("sbuf", [128, 4 * G], "float32"),
+    "diag": ("sbuf", [128, 4 * G], "float32"),
+    "part": ("sbuf", [128, 32], "float32"),
+    "turn": ("sbuf", [128, 32], "float32"),
     "vmax": ("sbuf", [128, 4], "float32"),
     "amax": ("sbuf", [128, 12], "float32"),
     "big": ("sbuf", [128, 4], "float32"),
@@ -32,9 +33,9 @@ SCRATCH = {
     "yb": ("sbuf", [128, N * NC], "float32"),
     "ps": ("psum", [128, 4096], "float32"),
 }
-SEMAPHORES = (["l_x", "l_wa", "l_wb", "l_w2", "q_x", "q_w0", "q_w1", "q_w2", "q_w3", "q_v", "q_h",
-               "z0", "z1", "z2", "z3", "ones", "zero", "ident", "part", "vmax", "diag", "bc", "own",
-               "big", "s", "hv", "hsc", "m_in", "sent", "st", "rm_in", "rc_in", "rp_in"]
+SEMAPHORES = (["l_x", "l_w0", "l_w1", "l_w2", "l_w3", "l_v", "q_x", "q_w0", "q_w1", "q_w2", "q_w3", "q_v", "q_h",
+               "z0", "z1", "z2", "z3", "ones", "zero", "pick", "part", "turn", "vmax", "diag", "bc", "own",
+               "big", "s", "hv", "hsc", "in_m", "sent", "st", "st2", "relay_m", "relay_c", "relay_p"]
               + ["arr%d" % j for j in range(N)] + ["y%d" % j for j in range(N)] + ["c%d" % j for j in range(N)])
 
 
@@ -42,41 +43,40 @@ def count(mask):
     return bin(mask).count("1")
 
 
-def routes(T, topo, r):
+def plan(T, topo, r):
     me = T.cores[r]
     others = [j for j in range(N) if j != r]
     near = [j for j in others if topo.may_write(me, T.cores[j])]
     far = [j for j in others if j not in near]
+    ring = sorted(near + [r])
+    i = ring.index(r)
+    near = [ring[(i + k) % len(ring)] for k in range(1, len(ring))]
     chip = [c for c in range(256) if c != me and topo.host(c) == topo.host(me) and topo.chip(c) == topo.chip(me)]
     rel = [c for c in chip if all(topo.may_write(c, T.cores[j]) for j in far)]
     a = [c for c in rel if topo.die(c) == topo.die(me)]
     b = [c for c in rel if topo.die(c) != topo.die(me)]
-    if sorted(near + [r]).index(r) % 2:
-        a, b = b, a
+    N_, F = [T.cores[j] for j in near], [T.cores[j] for j in far]
+    off = topo.mask(me, N_[0])
+    on = topo.mask(me, rel[0])
+    side = on & ~off
     if len(far) > 2:
-        m = list(zip([a[0], b[0], a[1], b[1]], [[j] for j in far]))
-        c = [(a[0], far[:2]), (b[0], far[2:])]
-        p = [(b[1], far[:2]), (a[1], far[2:])]
+        calls = [[("m", [a[0], b[0], a[1], b[1]], side)], [("m", N_, off)],
+                 [("c", b, on)], [("p", a, on)], [("c", N_, off)], [("p", N_, off)]]
+        relays = {a[0]: [("m", F[:1], off), ("p", F[:2], off)], a[1]: [("m", F[1:2], off), ("p", F[2:], off)],
+                  b[0]: [("m", F[2:3], off), ("c", F[2:], off)], b[1]: [("m", F[3:], off), ("c", F[:2], off)]}
     else:
-        m = [(a[0], far[:1]), (b[0], far[1:])]
-        c = [(a[0], far)]
-        p = [(b[0], far)]
-    return near, far, m, c, p
+        A, B = (b[0], a[0]) if i % 2 else (a[0], b[0])
+        calls = [[("m", [A, B], side)], [("m", N_, off)],
+                 [("c", [A], side), ("c", N_[:1], off)], [("p", [B], side), ("p", N_, off)]]
+        calls += [[("c", [d], off)] for d in N_[1:]]
+        relays = {A: [("m", F[:1], off), ("c", F, off)], B: [("m", F[1:], off), ("p", F, off)]}
+    return near, far, calls, relays
 
 
-def dst(topo, src, d):
-    rid, pid = topo.addr(d, src)
-    return DstId(rid=rid, pnc=pid)
-
-
-def xfer(topo, core, src, dests, mask, sem):
-    return RemoteDMATransfer(dst_ids=[dst(topo, core, d) for d, _ in dests], dma_engine_mask=mask, remote_sem=sem,
-                             srcs=[src], dsts=[v for _, v in dests])
-
-
-def mcol(T, d, r):
-    k = 4 + (r if r < d else r - 1)
-    return T.amax[:, k:k + 1]
+def landed(T, topo, r, core, kinds):
+    _, _, calls, relays = plan(T, topo, r)
+    ts = [t for call in calls for t in call] + [t for k in relays for t in relays[k]]
+    return sum(count(mask) for kind, cores, mask in ts if kind in kinds for c in cores if c == core)
 
 
 def codes(v):
@@ -87,39 +87,38 @@ def blk(t, j):
     return t[:, NC * j:NC * j + NC]
 
 
+def xfer(T, topo, core, r, src, kind, cores, mask):
+    ids, views = [], []
+    for d in cores:
+        rid, pid = topo.addr(d, core)
+        ids.append(DstId(rid=rid, pnc=pid))
+        q = T.rank_of(d)
+        if kind == "m":
+            k = 4 + (r if q is None or r < q else r - 1)
+            views.append(T.rm[:, 0:1] if q is None else T.amax[:, k:k + 1])
+        elif kind == "c":
+            views.append(codes(T.rc[:, :] if q is None else blk(T.lc, r)))
+        else:
+            views.append(T.rp[:, :] if q is None else blk(T.lp, r))
+    if T.rank_of(cores[0]) is None:
+        sem = T.sem["relay_" + kind]
+    else:
+        sem = T.sem.in_m if kind == "m" else T.sem["arr%d" % r]
+    return RemoteDMATransfer(dst_ids=ids, dma_engine_mask=mask, remote_sem=sem, srcs=[src], dsts=views)
+
+
 def relay_program(g, core, T, topo):
     for r in range(N):
-        near, far, m, c, p = routes(T, topo, r)
-        me = T.cores[r]
+        relays = plan(T, topo, r)[3]
+        if core not in relays:
+            continue
         sent = 0
-        on = topo.mask(me, core) if me != core else 0
-        for kind, table in (("m", m), ("c", c), ("p", p)):
-            for rc, dests in table:
-                if rc != core:
-                    continue
-                off = topo.mask(core, T.cores[dests[0]])
-                if kind == "m":
-                    g.wait_ge(T.sem.rm_in, count(hand_mask(T, topo, r, core)))
-                    t = xfer(topo, core, T.rm[:, 0:1], [(T.cores[d], mcol(T, d, r)) for d in dests], off, T.sem.m_in)
-                elif kind == "c":
-                    g.wait_ge(T.sem.rc_in, count(hand_mask(T, topo, r, core)))
-                    t = xfer(topo, core, codes(T.rc[:, :]), [(T.cores[d], codes(blk(T.lc, r))) for d in dests], off,
-                             T.sem["arr%d" % r])
-                else:
-                    g.wait_ge(T.sem.rp_in, count(hand_mask(T, topo, r, core)))
-                    t = xfer(topo, core, T.rp[:, :], [(T.cores[d], blk(T.lp, r)) for d in dests], off,
-                             T.sem["arr%d" % r])
-                g.remote_dma_fused([t], local_sem=T.sem.sent)
-                sent += count(off)
-        if sent:
-            g.wait_ge(T.sem.sent, sent)
-
-
-def hand_mask(T, topo, r, relay):
-    near, far, m, c, p = routes(T, topo, r)
-    on = topo.mask(T.cores[r], relay)
-    off = topo.mask(T.cores[r], T.cores[near[0]])
-    return on if len(far) > len(near) else on & ~off
+        src = {"m": T.rm[:, 0:1], "c": codes(T.rc[:, :]), "p": T.rp[:, :]}
+        for kind, cores, mask in relays[core]:
+            g.wait_ge(T.sem["relay_" + kind], landed(T, topo, r, core, kind))
+            g.remote_dma_fused([xfer(T, topo, core, r, src[kind], kind, cores, mask)], local_sem=T.sem.sent)
+            sent += count(mask)
+        g.wait_ge(T.sem.sent, sent)
 
 
 def rank_program(g, core, T, topo):
@@ -128,26 +127,28 @@ def rank_program(g, core, T, topo):
         relay_program(g, core, T, topo)
         return
     S = T.sem
-    near, far, m, c, p = routes(T, topo, rank)
-    off = topo.mask(core, T.cores[near[0]])
-    hand = hand_mask(T, topo, rank, m[0][0])
-    order = [rank] + near + far
+    near, far, calls, _ = plan(T, topo, rank)
+    order = [rank] + near[::-1] + far
     X, V, A, E, Y = AxisListType.X, g.vector, g.scalar, g.tensor, g.sync
     mult, mx = AluOpType.mult, AluOpType.max
-    half = G // 2 * W
+    sent = sum(count(mask) for call in calls for kind, _, mask in call)
 
     Y.dma_start(T.xb[:, :], T.x[:, :]).then_inc(S.l_x, 16)
-    A.dma_start(T.w1b[:, 0:half], T.w1[:, 0:half]).then_inc(S.l_wa, 16)
-    Y.dma_start(T.w1b[:, half:2 * half], T.w1[:, half:2 * half]).then_inc(S.l_wb, 16)
-    Y.wait_ge(S.l_wb, 16)
-    Y.dma_start(T.w2b[:, :], T.w2[:, :]).then_inc(S.l_w2, 16)
+    for i in range(G):
+        (A if i % 2 == 0 else Y).dma_start(T.w1b[:, W * i:W * i + W],
+                                           T.w1[:, W * i:W * i + W]).then_inc(S["l_w%d" % i], 16)
+    Y.wait_ge(S.l_w3, 16)
+    Y.dma_start(T.w2b[:, :], T.w2[:, :]).then_inc(S.l_v, 16)
 
     V.memset(T.ones[:, :], 1.0).then_inc(S.ones, 1)
     V.memset(T.amax[:, 0:4], 0.0).then_inc(S.zero, 1)
+    V.memset(T.part[:, :], 0.0).then_inc(S.zero, 1)
     g.wait_ge(S.ones, 1)
-    g.affine_select(T.ident[:, :], T.ones[:, :], [[-1, 128]], AluOpType.is_equal, 0.0, 0, 1).then_inc(S.ident, 1)
+    g.affine_select(T.pick[:, :], T.ones[:, 0:4 * G], [[-32, 4], [-1, G]], AluOpType.is_equal, 0.0, 0,
+                    1).then_inc(S.pick, 1)
 
     def quant_w(i):
+        V.wait_ge(S["l_w%d" % i], 16)
         V.quantize_mx(blk(T.wq, i), blk(T.ws, i), T.w1b[:, W * i:W * i + W]).then_inc(S["q_w%d" % i], 1)
 
     def reduce_z(i):
@@ -157,21 +158,22 @@ def rank_program(g, core, T, topo):
 
     V.wait_ge(S.l_x, 16)
     V.quantize_mx(T.xq[:, :], T.xs[:, :], T.xb[:, :]).then_inc(S.q_x, 1)
-    V.wait_ge(S.l_wa, 16)
+    V.wait_ge(S.zero, 2)
     quant_w(0)
     quant_w(1)
     reduce_z(0)
-    reduce_z(1)
-    V.wait_ge(S.l_wb, 16)
     quant_w(2)
+    reduce_z(1)
     quant_w(3)
     reduce_z(2)
     reduce_z(3)
     V.wait_ge(S.part, G)
-    V.tensor_reduce(T.vmax[:, 0:1], T.part[:, 0:G], X, mx).then_inc(S.vmax, 1)
+    V.transpose(T.turn[:, :], T.part[:, :]).then_inc(S.turn, 1)
+    V.wait_ge(S.turn, 1)
+    V.tensor_reduce(T.vmax[:, 0:1], T.turn[:, :], X, mx).then_inc(S.vmax, 1)
     V.wait_ge(S.vmax, 1)
-    V.wait_ge(S.ident, 1)
-    V.tensor_scalar(T.diag[:, :], T.ident[:, :], T.vmax[:, 0:1], None, mult).then_inc(S.diag, 1)
+    V.wait_ge(S.pick, 1)
+    V.tensor_scalar(T.diag[:, :], T.pick[:, :], T.vmax[:, 0:1], None, mult).then_inc(S.diag, 1)
 
     E.wait_ge(S.q_x, 1)
     for i in range(G):
@@ -180,25 +182,26 @@ def rank_program(g, core, T, topo):
                     True, True).then_inc(S["z%d" % i], 1)
     E.wait_ge(S.ones, 1)
     E.wait_ge(S.diag, 1)
-    E.matmul(T.ps[:, 2048:2048 + 128], T.ones[:, :], T.diag[:, :], True, True).then_inc(S.bc, 1)
+    E.matmul(T.ps[:, 2048:2048 + 4 * G], T.ones[:, :], T.diag[:, :], True, True).then_inc(S.bc, 1)
 
     V.wait_ge(S.bc, 1)
-    V.wait_ge(S.zero, 1)
-    V.tensor_reduce(T.amax[:, 0:1], T.ps[:, 2048:2048 + 128], X, mx).then_inc(S.own, 1)
+    V.tensor_reduce(T.amax[:, 0:1], T.ps[:, 2048:2048 + 4 * G], X, mx).then_inc(S.own, 1)
 
-    sent = 0
+    src = {"m": T.amax[:, 0:1], "c": codes(T.hq[:, :]), "p": T.hs[:, :]}
     g.wait_ge(S.own, 1)
-    g.remote_dma_fused([xfer(topo, core, T.amax[:, 0:1], [(k, T.rm[:, 0:1]) for k, _ in m], hand, S.rm_in)],
-                       local_sem=S.sent)
-    g.remote_dma_fused([xfer(topo, core, T.amax[:, 0:1], [(T.cores[d], mcol(T, d, rank)) for d in near], off, S.m_in)],
-                       local_sem=S.sent)
-    sent += count(hand) + count(off)
+    ready = False
+    for call in calls:
+        if call[0][0] != "m" and not ready:
+            g.wait_ge(S.q_h, 1)
+            ready = True
+        g.remote_dma_fused([xfer(T, topo, core, rank, src[kind], kind, cores, mask) for kind, cores, mask in call],
+                           local_sem=S.sent)
 
-    V.wait_ge(S.l_w2, 16)
+    V.wait_ge(S.l_v, 16)
     V.quantize_mx(T.vq[:, :], T.vs[:, :], T.w2b[:, :]).then_inc(S.q_v, 1)
 
     V.wait_ge(S.own, 1)
-    V.wait_ge(S.m_in, sum(count(topo.mask(T.cores[j], core)) for j in near) + sum(count(off) for j in far))
+    V.wait_ge(S.in_m, sum(landed(T, topo, j, core, "m") for j in order[1:]))
     V.tensor_reduce(T.big[:, 0:1], T.amax[:, 0:4 + N - 1], X, mx).then_inc(S.big, 1)
     V.wait_ge(S.big, 1)
     V.reciprocal(T.s[:, 0:1], T.big[:, 0:1]).then_inc(S.s, 1)
@@ -217,33 +220,24 @@ def rank_program(g, core, T, topo):
     Y.wait_ge(S.hsc, 2)
     Y.dma_start(T.h[:, :], T.hb[:, :]).then_inc(S.st, 16)
 
-    g.wait_ge(S.q_h, 1)
-    hq, hs = codes(T.hq[:, :]), T.hs[:, :]
-    arr = S["arr%d" % rank]
-    tc = xfer(topo, core, hq, [(k, codes(T.rc[:, :])) for k, _ in c], hand, S.rc_in)
-    tp = xfer(topo, core, hs, [(k, T.rp[:, :]) for k, _ in p], hand, S.rp_in)
-    nc = xfer(topo, core, hq, [(T.cores[d], codes(blk(T.lc, rank))) for d in near], off, arr)
-    np_ = xfer(topo, core, hs, [(T.cores[d], blk(T.lp, rank)) for d in near], off, arr)
-    calls = [[tc, nc], [tp, np_]] if hand & off == 0 else [[tc], [tp], [nc], [np_]]
-    for call in calls:
-        g.remote_dma_fused(call, local_sem=S.sent)
-    sent += 2 * count(hand) + 2 * count(off)
-
     E.wait_ge(S.q_v, 1)
     E.wait_ge(S.q_h, 1)
     for k, j in enumerate(order):
         bank = 512 * ((5 + k) % 8)
         if j != rank:
-            E.wait_ge(S["arr%d" % j], 2 * count(off))
+            E.wait_ge(S["arr%d" % j], landed(T, topo, j, core, "cp"))
         qc, qs = (T.hq[:, :], T.hs[:, :]) if j == rank else (blk(T.lc, j), blk(T.lp, j))
         E.matmul_mx(T.ps[:, bank:bank + NC], T.vq[:, :], T.vs[:, :], qc, qs, True, True).then_inc(S["y%d" % k], 1)
-        q = V if k % 2 == 0 else A
-        q.wait_ge(S["y%d" % k], 1)
         if k % 2 == 0:
+            V.wait_ge(S["y%d" % k], 1)
             V.tensor_copy(blk(T.yb, j), T.ps[:, bank:bank + NC]).then_inc(S["c%d" % k], 1)
+            Y.wait_ge(S["c%d" % k], 1)
+            Y.dma_start(blk(T.y, j), blk(T.yb, j)).then_inc(S.st, 16)
         else:
+            A.wait_ge(S["y%d" % k], 1)
             A.activation(blk(T.yb, j), T.ps[:, bank:bank + NC], ActivationFunctionType.Copy).then_inc(S["c%d" % k], 1)
-        Y.wait_ge(S["c%d" % k], 1)
-        Y.dma_start(blk(T.y, j), blk(T.yb, j)).then_inc(S.st, 16)
-    Y.wait_ge(S.st, 16 * (N + 1))
+            A.wait_ge(S["c%d" % k], 1)
+            A.dma_start(blk(T.y, j), blk(T.yb, j)).then_inc(S.st2, 16)
+    Y.wait_ge(S.st, 16 * (N // 2 + 1))
+    A.wait_ge(S.st2, 16 * (N // 2))
     g.wait_ge(S.sent, sent)

from concourse.bass import DstId, RemoteDMATransfer
from concourse.mybir import dt, AluOpType, AxisListType, ActivationFunctionType

N, NC, G = 6, 128, 4
W = 4 * NC
SCRATCH = {
    "xb": ("sbuf", [128, W], "bfloat16"),
    "w1b": ("sbuf", [128, G * W], "bfloat16"),
    "w2b": ("sbuf", [128, W], "bfloat16"),
    "xq": ("sbuf", [128, NC], "float8_e4m3fn_x4"),
    "xs": ("sbuf", [128, NC], "uint8"),
    "wq": ("sbuf", [128, G * NC], "float8_e4m3fn_x4"),
    "ws": ("sbuf", [128, G * NC], "uint8"),
    "vq": ("sbuf", [128, NC], "float8_e4m3fn_x4"),
    "vs": ("sbuf", [128, NC], "uint8"),
    "ones": ("sbuf", [128, 128], "float32"),
    "pick": ("sbuf", [128, 4 * G], "float32"),
    "diag": ("sbuf", [128, 4 * G], "float32"),
    "part": ("sbuf", [128, 32], "float32"),
    "turn": ("sbuf", [128, 32], "float32"),
    "vmax": ("sbuf", [128, 4], "float32"),
    "amax": ("sbuf", [128, 12], "float32"),
    "big": ("sbuf", [128, 4], "float32"),
    "s": ("sbuf", [128, 4], "float32"),
    "hb": ("sbuf", [128, W], "bfloat16"),
    "hq": ("sbuf", [128, NC], "float8_e4m3fn_x4"),
    "hs": ("sbuf", [128, NC], "uint8"),
    "lc": ("sbuf", [128, N * NC], "float8_e4m3fn_x4"),
    "lp": ("sbuf", [128, N * NC], "uint8"),
    "rm": ("sbuf", [128, 4], "float32"),
    "rc": ("sbuf", [128, NC], "float8_e4m3fn_x4"),
    "rp": ("sbuf", [128, NC], "uint8"),
    "yb": ("sbuf", [128, N * NC], "float32"),
    "ps": ("psum", [128, 4096], "float32"),
}
SEMAPHORES = (["l_x", "l_w0", "l_w1", "l_w2", "l_w3", "l_v", "q_x", "q_w0", "q_w1", "q_w2", "q_w3", "q_v", "q_h",
               "z0", "z1", "z2", "z3", "ones", "zero", "pick", "part", "turn", "vmax", "diag", "bc", "own",
               "big", "s", "hv", "hsc", "in_m", "sent", "st", "st2", "relay_m", "relay_c", "relay_p"]
              + ["arr%d" % j for j in range(N)] + ["y%d" % j for j in range(N)] + ["c%d" % j for j in range(N)])


def count(mask):
    return bin(mask).count("1")


def plan(T, topo, r):
    me = T.cores[r]
    others = [j for j in range(N) if j != r]
    near = [j for j in others if topo.may_write(me, T.cores[j])]
    far = [j for j in others if j not in near]
    ring = sorted(near + [r])
    i = ring.index(r)
    near = [ring[(i + k) % len(ring)] for k in range(1, len(ring))]
    chip = [c for c in range(256) if c != me and topo.host(c) == topo.host(me) and topo.chip(c) == topo.chip(me)]
    rel = [c for c in chip if all(topo.may_write(c, T.cores[j]) for j in far)]
    a = [c for c in rel if topo.die(c) == topo.die(me)]
    b = [c for c in rel if topo.die(c) != topo.die(me)]
    N_, F = [T.cores[j] for j in near], [T.cores[j] for j in far]
    off = topo.mask(me, N_[0])
    on = topo.mask(me, rel[0])
    side = on & ~off
    if len(far) > 2:
        calls = [[("m", [a[0], b[0], a[1], b[1]], side)], [("m", N_, off)],
                 [("c", b, on)], [("p", a, on)], [("c", N_, off)], [("p", N_, off)]]
        relays = {a[0]: [("m", F[:1], off), ("p", F[:2], off)], a[1]: [("m", F[1:2], off), ("p", F[2:], off)],
                  b[0]: [("m", F[2:3], off), ("c", F[2:], off)], b[1]: [("m", F[3:], off), ("c", F[:2], off)]}
    else:
        A, B = (b[0], a[0]) if i % 2 else (a[0], b[0])
        calls = [[("m", [A, B], side)], [("m", N_, off)],
                 [("c", [A], side), ("c", N_[:1], off)], [("p", [B], side), ("p", N_, off)]]
        calls += [[("c", [d], off)] for d in N_[1:]]
        relays = {A: [("m", F[:1], off), ("c", F, off)], B: [("m", F[1:], off), ("p", F, off)]}
    return near, far, calls, relays


def landed(T, topo, r, core, kinds):
    _, _, calls, relays = plan(T, topo, r)
    ts = [t for call in calls for t in call] + [t for k in relays for t in relays[k]]
    return sum(count(mask) for kind, cores, mask in ts if kind in kinds for c in cores if c == core)


def codes(v):
    return v.bitcast(dt.uint8)


def blk(t, j):
    return t[:, NC * j:NC * j + NC]


def xfer(T, topo, core, r, src, kind, cores, mask):
    ids, views = [], []
    for d in cores:
        rid, pid = topo.addr(d, core)
        ids.append(DstId(rid=rid, pnc=pid))
        q = T.rank_of(d)
        if kind == "m":
            k = 4 + (r if q is None or r < q else r - 1)
            views.append(T.rm[:, 0:1] if q is None else T.amax[:, k:k + 1])
        elif kind == "c":
            views.append(codes(T.rc[:, :] if q is None else blk(T.lc, r)))
        else:
            views.append(T.rp[:, :] if q is None else blk(T.lp, r))
    if T.rank_of(cores[0]) is None:
        sem = T.sem["relay_" + kind]
    else:
        sem = T.sem.in_m if kind == "m" else T.sem["arr%d" % r]
    return RemoteDMATransfer(dst_ids=ids, dma_engine_mask=mask, remote_sem=sem, srcs=[src], dsts=views)


def relay_program(g, core, T, topo):
    for r in range(N):
        relays = plan(T, topo, r)[3]
        if core not in relays:
            continue
        sent = 0
        src = {"m": T.rm[:, 0:1], "c": codes(T.rc[:, :]), "p": T.rp[:, :]}
        for kind, cores, mask in relays[core]:
            g.wait_ge(T.sem["relay_" + kind], landed(T, topo, r, core, kind))
            g.remote_dma_fused([xfer(T, topo, core, r, src[kind], kind, cores, mask)], local_sem=T.sem.sent)
            sent += count(mask)
        g.wait_ge(T.sem.sent, sent)


def rank_program(g, core, T, topo):
    rank = T.rank_of(core)
    if rank is None:
        relay_program(g, core, T, topo)
        return
    S = T.sem
    near, far, calls, _ = plan(T, topo, rank)
    order = [rank] + near[::-1] + far
    X, V, A, E, Y = AxisListType.X, g.vector, g.scalar, g.tensor, g.sync
    mult, mx = AluOpType.mult, AluOpType.max
    sent = sum(count(mask) for call in calls for kind, _, mask in call)

    Y.dma_start(T.xb[:, :], T.x[:, :]).then_inc(S.l_x, 16)
    for i in range(G):
        (A if i % 2 == 0 else Y).dma_start(T.w1b[:, W * i:W * i + W],
                                           T.w1[:, W * i:W * i + W]).then_inc(S["l_w%d" % i], 16)
    Y.wait_ge(S.l_w3, 16)
    Y.dma_start(T.w2b[:, :], T.w2[:, :]).then_inc(S.l_v, 16)

    V.memset(T.ones[:, :], 1.0).then_inc(S.ones, 1)
    V.memset(T.amax[:, 0:4], 0.0).then_inc(S.zero, 1)
    V.memset(T.part[:, :], 0.0).then_inc(S.zero, 1)
    g.wait_ge(S.ones, 1)
    g.affine_select(T.pick[:, :], T.ones[:, 0:4 * G], [[-32, 4], [-1, G]], AluOpType.is_equal, 0.0, 0,
                    1).then_inc(S.pick, 1)

    def quant_w(i):
        V.wait_ge(S["l_w%d" % i], 16)
        V.quantize_mx(blk(T.wq, i), blk(T.ws, i), T.w1b[:, W * i:W * i + W]).then_inc(S["q_w%d" % i], 1)

    def reduce_z(i):
        V.wait_ge(S["z%d" % i], 1)
        V.tensor_reduce(T.part[:, i:i + 1], T.ps[:, 512 * i:512 * i + NC], X, mx,
                        apply_absolute_value=True).then_inc(S.part, 1)

    V.wait_ge(S.l_x, 16)
    V.quantize_mx(T.xq[:, :], T.xs[:, :], T.xb[:, :]).then_inc(S.q_x, 1)
    V.wait_ge(S.zero, 2)
    quant_w(0)
    quant_w(1)
    reduce_z(0)
    quant_w(2)
    reduce_z(1)
    quant_w(3)
    reduce_z(2)
    reduce_z(3)
    V.wait_ge(S.part, G)
    V.transpose(T.turn[:, :], T.part[:, :]).then_inc(S.turn, 1)
    V.wait_ge(S.turn, 1)
    V.tensor_reduce(T.vmax[:, 0:1], T.turn[:, :], X, mx).then_inc(S.vmax, 1)
    V.wait_ge(S.vmax, 1)
    V.wait_ge(S.pick, 1)
    V.tensor_scalar(T.diag[:, :], T.pick[:, :], T.vmax[:, 0:1], None, mult).then_inc(S.diag, 1)

    E.wait_ge(S.q_x, 1)
    for i in range(G):
        E.wait_ge(S["q_w%d" % i], 1)
        E.matmul_mx(T.ps[:, 512 * i:512 * i + NC], blk(T.wq, i), blk(T.ws, i), T.xq[:, :], T.xs[:, :],
                    True, True).then_inc(S["z%d" % i], 1)
    E.wait_ge(S.ones, 1)
    E.wait_ge(S.diag, 1)
    E.matmul(T.ps[:, 2048:2048 + 4 * G], T.ones[:, :], T.diag[:, :], True, True).then_inc(S.bc, 1)

    V.wait_ge(S.bc, 1)
    V.tensor_reduce(T.amax[:, 0:1], T.ps[:, 2048:2048 + 4 * G], X, mx).then_inc(S.own, 1)

    src = {"m": T.amax[:, 0:1], "c": codes(T.hq[:, :]), "p": T.hs[:, :]}
    g.wait_ge(S.own, 1)
    ready = False
    for call in calls:
        if call[0][0] != "m" and not ready:
            g.wait_ge(S.q_h, 1)
            ready = True
        g.remote_dma_fused([xfer(T, topo, core, rank, src[kind], kind, cores, mask) for kind, cores, mask in call],
                           local_sem=S.sent)

    V.wait_ge(S.l_v, 16)
    V.quantize_mx(T.vq[:, :], T.vs[:, :], T.w2b[:, :]).then_inc(S.q_v, 1)

    V.wait_ge(S.own, 1)
    V.wait_ge(S.in_m, sum(landed(T, topo, j, core, "m") for j in order[1:]))
    V.tensor_reduce(T.big[:, 0:1], T.amax[:, 0:4 + N - 1], X, mx).then_inc(S.big, 1)
    V.wait_ge(S.big, 1)
    V.reciprocal(T.s[:, 0:1], T.big[:, 0:1]).then_inc(S.s, 1)
    V.wait_ge(S.s, 1)
    A.wait_ge(S.s, 1)
    for b in (0, 1):
        V.tensor_scalar(T.hb[:, b:W:G], T.ps[:, 512 * b:512 * b + NC], T.s[:, 0:1], None, mult).then_inc(S.hv, 1)
    for b in (2, 3):
        A.wait_ge(S["z%d" % b], 1)
        A.activation(T.hb[:, b:W:G], T.ps[:, 512 * b:512 * b + NC], ActivationFunctionType.Copy,
                     scale=T.s[:, 0:1]).then_inc(S.hsc, 1)
    V.wait_ge(S.hv, 2)
    V.wait_ge(S.hsc, 2)
    V.quantize_mx(T.hq[:, :], T.hs[:, :], T.hb[:, :]).then_inc(S.q_h, 1)
    Y.wait_ge(S.hv, 2)
    Y.wait_ge(S.hsc, 2)
    Y.dma_start(T.h[:, :], T.hb[:, :]).then_inc(S.st, 16)

    E.wait_ge(S.q_v, 1)
    E.wait_ge(S.q_h, 1)
    for k, j in enumerate(order):
        bank = 512 * ((5 + k) % 8)
        if j != rank:
            E.wait_ge(S["arr%d" % j], landed(T, topo, j, core, "cp"))
        qc, qs = (T.hq[:, :], T.hs[:, :]) if j == rank else (blk(T.lc, j), blk(T.lp, j))
        E.matmul_mx(T.ps[:, bank:bank + NC], T.vq[:, :], T.vs[:, :], qc, qs, True, True).then_inc(S["y%d" % k], 1)
        if k % 2 == 0:
            V.wait_ge(S["y%d" % k], 1)
            V.tensor_copy(blk(T.yb, j), T.ps[:, bank:bank + NC]).then_inc(S["c%d" % k], 1)
            Y.wait_ge(S["c%d" % k], 1)
            Y.dma_start(blk(T.y, j), blk(T.yb, j)).then_inc(S.st, 16)
        else:
            A.wait_ge(S["y%d" % k], 1)
            A.activation(blk(T.yb, j), T.ps[:, bank:bank + NC], ActivationFunctionType.Copy).then_inc(S["c%d" % k], 1)
            A.wait_ge(S["c%d" % k], 1)
            A.dma_start(blk(T.y, j), blk(T.yb, j)).then_inc(S.st2, 16)
    Y.wait_ge(S.st, 16 * (N // 2 + 1))
    A.wait_ge(S.st2, 16 * (N // 2))
    g.wait_ge(S.sent, sent)
